import numpy as np
import ml_dtypes


def mxq(x, axis, fmt="e4m3"):
    dtype, down = {"e4m3": (ml_dtypes.float8_e4m3fn, 7), "e5m2": (ml_dtypes.float8_e5m2, 14)}[fmt]
    v = np.moveaxis(np.asarray(x, np.float32).astype(ml_dtypes.bfloat16).astype(np.float64), axis, -1)
    blocks = v.reshape(v.shape[:-1] + (-1, 32))
    amax = np.abs(blocks).max(-1, keepdims=True)
    byte = np.maximum(np.where(amax > 0, np.frexp(amax)[1] - 1 + 127, 0) - down, 1)
    scale = np.exp2(byte - 127.0)
    codes = (blocks / scale).astype(np.float32).astype(dtype).astype(np.float64)
    return np.moveaxis((codes * scale).reshape(v.shape), -1, axis)


WIDE = False


def mx_kscale(k):
    if not WIDE:
        return np.ones(k)
    levels = np.array([10, -10, 5, -5, 0])
    if k % 512:
        return np.exp2(np.random.permutation(np.resize(levels, k // 32))).repeat(32)
    a = np.empty((k // 512, 16))
    for p in range(k // 512):
        a[p, :8] = np.random.permutation(np.resize(levels, 8))
        for g in range(8):
            far = levels[np.abs(levels - a[p, g]) >= 10]
            a[p, g + 8] = far[np.random.randint(len(far))]
    return np.exp2(a.ravel()).repeat(32)


def f64(x):
    return np.asarray(x).astype(np.float64)


def striped(idx):
    return np.tile(idx.reshape(-1, 16).T, (8, 1)).astype(np.uint16)


def unstriped(offs):
    return offs[:16].T.reshape(-1).astype(np.int64)


E2M1 = np.array([0.0, 0.5, 1.0, 1.5, 2.0, 3.0, 4.0, 6.0, -0.0, -0.5, -1.0, -1.5, -2.0, -3.0, -4.0, -6.0])


def pack_weight(w, fmt):
    k, n = w.shape
    w = f64(np.asarray(w, np.float32).astype(ml_dtypes.bfloat16)).reshape(k // 32, 32, n)
    amax = np.abs(w).max(1)
    if fmt == "e4m3":
        byte = np.frexp(amax)[1] - 1 + 127 - 7
    else:
        mant, ex = np.frexp(amax / 6.0)
        byte = np.where(mant > 0.5, ex, ex - 1) + 127
    byte = np.clip(np.where(amax > 0, byte, 1), 1, 254)
    scaled = (w * np.exp2(127.0 - byte)[:, None, :]).reshape(k, n).astype(np.float32)
    by_word = np.ascontiguousarray(scaled.reshape(k // 512, 128, 4, n).transpose(0, 1, 3, 2))
    if fmt == "e4m3":
        words = by_word.astype(ml_dtypes.float8_e4m3fn).view(np.uint8)
    else:
        c = by_word.astype(ml_dtypes.float4_e2m1fn).view(np.uint8) & 0xF
        words = (c[..., 0::2] | (c[..., 1::2] << 4)).reshape(k // 512, 128, 2 * n)
    return np.ascontiguousarray(words), np.ascontiguousarray(byte.astype(np.uint8).reshape(k // 512, 16, n))


def unpack_weight(words, scales, fmt):
    g, _, n = scales.shape
    words = np.ascontiguousarray(words).reshape(g, 128, n, -1)
    if fmt == "e4m3":
        vals = words.view(ml_dtypes.float8_e4m3fn).astype(np.float64)
    else:
        nib = np.empty((g, 128, n, 4), np.uint8)
        nib[..., 0::2] = words & 0xF
        nib[..., 1::2] = words >> 4
        vals = E2M1[nib]
    vals = vals * np.repeat(np.exp2(scales.astype(np.float64) - 127.0), 8, axis=1)[..., None]
    return vals.transpose(0, 1, 3, 2).reshape(g * 512, n)


def gelu(v):
    return 0.5 * v * (1.0 + np.tanh(np.sqrt(2.0 / np.pi) * (v + 0.044715 * v**3)))


def bf(x):
    return np.asarray(x, np.float32).astype(ml_dtypes.bfloat16)


def planes(Y):
    n, m = Y.shape
    b = f64(bf(Y)).reshape(n // 32, 32, m)
    amax = np.abs(b).max(1)
    byte = np.clip(np.where(amax > 0, np.frexp(amax)[1] - 1 + 127 - 7, 1), 1, 254)
    codes = (b * np.exp2(127.0 - byte)[:, None, :]).reshape(n, m).astype(np.float32).astype(ml_dtypes.float8_e4m3fn).view(np.uint8)
    words = codes.reshape(n // 512, 128, 4, m).transpose(0, 1, 3, 2)
    return np.ascontiguousarray(words), np.ascontiguousarray(byte.astype(np.uint8).reshape(n // 512, 16, m))


K, H, T, S, P = 1536, 512, 4096, 1024, 512


def setup_inputs():
    n = np.random.standard_normal
    s = mx_kscale(K)[:, None]
    u = mx_kscale(H)[:, None]
    size = np.exp(0.8 * n(H))
    d = {}
    d["tab_words"], d["tab_scales"] = pack_weight(n((K, T)) * s, "e4m3")
    d["w1"] = (0.45 * n((K, H)) / K**0.5 / s * np.sqrt(size)).astype(np.float32)
    d["w2_words"], d["w2_scales"] = pack_weight(0.45 * n((K, H)) / K**0.5 / s * np.sqrt(size), "e2m1")
    d["gain"] = (np.random.uniform(0.5, 1.5, H) / size * u[:, 0]).astype(np.float32)
    d["w3"] = (n((H, H)) / H**0.5 / u * size).astype(np.float32)
    d["offs"] = striped(np.random.permutation(T)[:S])
    d["pos1"] = striped(np.random.permutation(S)[:P])
    d["pos2"] = striped(np.random.permutation(S)[:P])
    return d


def reference(tab_words, tab_scales, w1, w2_words, w2_scales, gain, w3, offs, pos1, pos2):
    v = unpack_weight(tab_words, tab_scales, "e4m3")[:, unstriped(offs)]
    w2 = unpack_weight(w2_words, w2_scales, "e2m1")
    a = mxq(f64(w1), 0, "e4m3").T @ v
    b = w2.T @ v
    f = np.square(a - np.abs(b))
    h = f64(gain)[:, None] * f
    g2 = (mxq(f64(w3), 0, "e4m3").T @ mxq(h, 0, "e4m3")) + f
    y = np.tanh(g2[:, unstriped(pos1)]) - g2[:, unstriped(pos2)]
    words, scales = planes(y)
    return y, words, scales

@@ -1,0 +1,340 @@
+from contextlib import ExitStack
+
+import concourse.mybir as mybir
+
+K, H, T, S, NP = 1536, 512, 4096, 1024, 512
+FLOPS = 2 * (2 * K * H * S + H * H * S)
+
+F32 = mybir.dt.float32
+BF16 = mybir.dt.bfloat16
+I32 = mybir.dt.int32
+U32 = mybir.dt.uint32
+U16 = mybir.dt.uint16
+U8 = mybir.dt.uint8
+FP8X4 = mybir.dt.float8_e4m3fn_x4
+FP4X4 = mybir.dt.float4_e2m1fn_x4
+ALU = mybir.AluOpType
+ACT = mybir.ActivationFunctionType
+
+P = 128
+PACK = 4
+K_PASS = P * PACK
+PASSES = K // K_PASS
+N_TILE = 512
+HALVES = S // N_TILE
+QUADS = 4
+QUAD = 32
+LIVE = 4
+SHIFT_ROWS = 112
+
+
+def tile_list_hose_gauge_features_kernel(
+    tc, tab_words, tab_scales, w1, w2_words, w2_scales, gain, w3, offs, pos1, pos2, out_0, out_1, out_2
+):
+    nc = tc.nc
+    with ExitStack() as ctx:
+        lists = ctx.enter_context(tc.tile_pool(name="lists", bufs=1))
+        keep = ctx.enter_context(tc.tile_pool(name="keep", bufs=1))
+        ring = ctx.enter_context(tc.tile_pool(name="ring", bufs=2))
+        reuse = ctx.enter_context(tc.tile_pool(name="reuse", bufs=1))
+        psum = ctx.enter_context(tc.psum_pool(name="psum", bufs=1))
+
+        def held(shape, dtype, name):
+            return keep.tile(shape, dtype, name=name, align_bytes=64)
+
+        def placed(shape, dtype, name, kib):
+            return reuse.tile(shape, dtype, name=name, align_bytes=64, offset=kib * 1024)
+
+        offs_sb = lists.tile([P, S // 16], U16, name="offs_sb")
+        pos1_sb = lists.tile([P, NP // 16], U16, name="pos1_sb")
+        pos2_sb = lists.tile([P, NP // 16], U16, name="pos2_sb")
+
+        tab_scale_win = placed([P, T], U8, "tab_scale_win", 46)
+        w2_scale_raw = held([P, PASSES, H], U8, "w2_scale_raw")
+        v_planes = held([P, PASSES - 1, S], U8, "v_planes")
+        nc.vector.memset(tab_scale_win[:].bitcast(I32), 0)
+        nc.vector.memset(w2_scale_raw[:].rearrange("p a c -> p (a c)").bitcast(I32), 0)
+        nc.vector.memset(v_planes[:].rearrange("p a c -> p (a c)").bitcast(I32), 0)
+
+        tab_sb = [placed([P, T], I32, "tab%d" % a, 16 * a) for a in range(PASSES)]
+        w2_raw = held([P, PASSES, 2 * H], U8, "w2_raw")
+        gain_sb = held([P, PACK], F32, "gain_sb")
+        w1_raw = [placed([P, PACK, H], F32, "w1_raw%d" % a, 8 * a) for a in range(PASSES - 1)]
+        w1_last = [placed([P, PACK, H // 2], F32, "w1_last%d" % c, 16 + 4 * c) for c in range(2)]
+        w3_raw = placed([P, PACK, H], F32, "w3_raw", 24)
+
+        def load_table(a):
+            nc.sync.dma_start(out=tab_sb[a][:], in_=tab_words[a].rearrange("p t i -> p (t i)").bitcast(I32))
+
+        def w1_rows(a):
+            return w1[a * K_PASS : (a + 1) * K_PASS, :].rearrange("(p j) c -> p j c", j=PACK)
+
+        nc.sync.dma_start(offs_sb[:], offs)
+        nc.sync.dma_start(out=w2_raw[:].bitcast(I32), in_=w2_words.rearrange("a p c -> p a c").bitcast(I32))
+        load_table(0)
+        load_table(1)
+        nc.sync.dma_start(pos1_sb[:], pos1)
+        nc.sync.dma_start(pos2_sb[:], pos2)
+        for q in range(QUADS):
+            nc.gpsimd.dma_start(
+                out=tab_scale_win[QUAD * q : QUAD * q + LIVE * PASSES, :].bitcast(I32),
+                in_=tab_scales[:, LIVE * q : LIVE * (q + 1), :].bitcast(I32),
+            )
+        for q in range(QUADS):
+            nc.gpsimd.dma_start(
+                out=w2_scale_raw[QUAD * q : QUAD * q + LIVE, :, :].bitcast(I32),
+                in_=w2_scales[:, LIVE * q : LIVE * (q + 1), :].rearrange("a r c -> r a c").bitcast(I32),
+            )
+        nc.sync.dma_start(out=gain_sb[:], in_=gain.rearrange("(p t) -> p t", t=PACK))
+
+        w2_codes = held([P, PACK, PASSES, 2 * P], U8, "w2_codes")
+        nc.vector.tensor_copy(
+            out=w2_codes[:].rearrange("p t a (m b) -> p t a m b", b=2),
+            in_=w2_raw[:].rearrange("p a (m t b) -> p t a m b", t=PACK, b=2),
+        )
+        v_scale_packed = held([P, S], U8, "v_scale_packed")
+        nc.vector.tensor_copy(out=v_scale_packed[:], in_=tab_scale_win[:].indirect(offs_sb[:]))
+        for a in range(1, PASSES):
+            nc.scalar.dma_start(
+                out=v_planes[0:SHIFT_ROWS, a - 1, :].bitcast(I32),
+                in_=v_scale_packed[LIVE * a : LIVE * a + SHIFT_ROWS, :].bitcast(I32),
+            )
+        w2_planes = held([P, PACK, PASSES, P], U8, "w2_planes")
+        nc.vector.tensor_copy(
+            out=w2_planes[:],
+            in_=w2_scale_raw[:].rearrange("p a (m t) -> p t a m", t=PACK),
+        )
+
+        def v_plane(a, half):
+            cols = slice(half * N_TILE, (half + 1) * N_TILE)
+            return v_scale_packed[:, cols] if a == 0 else v_planes[:, a - 1, cols]
+
+        v_early = placed([P, (PASSES - 1) * S], U32, "v_early", 48)
+        v_last = held([P, S], U32, "v_last")
+        v_words = [v_early[:, a * S : (a + 1) * S] for a in range(PASSES - 1)] + [v_last[:]]
+        load_table(PASSES - 1)
+        for a in range(PASSES - 1):
+            nc.vector.tensor_copy(out=v_words[a], in_=tab_sb[a][:].bitcast(U32).indirect(offs_sb[:]))
+        for a in range(PASSES - 1):
+            nc.sync.dma_start(out=w1_raw[a][:], in_=w1_rows(a))
+        for c in range(2):
+            nc.sync.dma_start(out=w1_last[c][:], in_=w1_rows(PASSES - 1)[:, :, c * (H // 2) : (c + 1) * (H // 2)])
+        nc.sync.dma_start(out=w3_raw[:], in_=w3.rearrange("(p j) c -> p j c", j=PACK))
+        for half in range(HALVES):
+            nc.vector.tensor_copy(
+                out=v_last[:, half * N_TILE : (half + 1) * N_TILE],
+                in_=tab_sb[PASSES - 1][:]
+                .bitcast(U32)
+                .indirect(offs_sb[:, half * (N_TILE // 16) : (half + 1) * (N_TILE // 16)]),
+            )
+
+        def v_codes(a, half):
+            return v_words[a][:, half * N_TILE : (half + 1) * N_TILE].bitcast(FP8X4)
+
+        def bank(half, t):
+            return psum.tile([P, N_TILE], F32, name="bank", tag="bank%d_%d" % (half, t))
+
+        blocks = [(half, t) for half in range(HALVES) for t in range(PACK)]
+
+        b_acc = {blk: bank(*blk) for blk in blocks}
+        for a in range(PASSES):
+            for half, t in blocks:
+                nc.tensor.matmul_mx(
+                    out=b_acc[half, t][:],
+                    lhsT=w2_codes[:, t, a, :].bitcast(FP4X4),
+                    lhsT_scale=w2_planes[:, t, a, :],
+                    rhs=v_codes(a, half),
+                    rhs_scale=v_plane(a, half),
+                    start=(a == 0),
+                    stop=(a == PASSES - 1),
+                )
+        f_sb = {(half, t): held([P, N_TILE], F32, "f%d_%d" % (half, t)) for half, t in blocks}
+        for blk in blocks:
+            nc.scalar.activation(out=f_sb[blk][:], in_=b_acc[blk][:], func=ACT.Abs)
+
+        def dealt_views(grouped, raw, m0):
+            width = raw.shape[2] // PACK
+            return (
+                grouped[:, :, m0 : m0 + width, :].rearrange("p t m j -> p m t j"),
+                raw[:].rearrange("p j (m t) -> p m t j", t=PACK),
+            )
+
+        w1_codes = [held([P, H], U32, "w1_codes%d" % a) for a in range(PASSES)]
+        w1_planes = [held([P, H], U8, "w1_planes%d" % a) for a in range(PASSES)]
+        for a in range(PASSES):
+            grouped = ring.tile([P, PACK, P, PACK], BF16, name="w1_grouped", align_bytes=64)
+            pieces = [(w1_raw[a], 0)] if a < PASSES - 1 else [(w1_last[c], c * (P // 2)) for c in range(2)]
+            for raw, m0 in pieces:
+                dst, src = dealt_views(grouped, raw, m0)
+                if a == PASSES - 1 and m0 == 0:
+                    nc.scalar.copy(out=dst, in_=src)
+                else:
+                    nc.vector.tensor_copy(out=dst, in_=src)
+            if a < PASSES - 1:
+                nc.vector.quantize_mx(
+                    out=w1_codes[a][:].bitcast(FP8X4),
+                    scales=w1_planes[a][:],
+                    in_=grouped[:].rearrange("p t m j -> p (t m j)"),
+                )
+            else:
+                for u in range(2):
+                    nc.vector.quantize_mx(
+                        out=w1_codes[a][:, u * 2 * P : (u + 1) * 2 * P].bitcast(FP8X4),
+                        scales=w1_planes[a][:, u * 2 * P : (u + 1) * 2 * P],
+                        in_=grouped[:, 2 * u : 2 * u + 2].rearrange("p t m j -> p (t m j)"),
+                    )
+
+        a_acc = {blk: bank(*blk) for blk in blocks}
+
+        def a_pass(a, half):
+            for t in range(PACK):
+                nc.tensor.matmul_mx(
+                    out=a_acc[half, t][:],
+                    lhsT=w1_codes[a][:, t * P : (t + 1) * P].bitcast(FP8X4),
+                    lhsT_scale=w1_planes[a][:, t * P : (t + 1) * P],
+                    rhs=v_codes(a, half),
+                    rhs_scale=v_plane(a, half),
+                    start=(a == 0),
+                    stop=(a == PASSES - 1),
+                )
+
+        for half in range(HALVES):
+            a_pass(0, half)
+        for half in range(HALVES):
+            for a in range(1, PASSES):
+                a_pass(a, half)
+
+        w3_grouped = held([P, PACK, P, PACK], BF16, "w3_grouped")
+        dst, src = dealt_views(w3_grouped, w3_raw, 0)
+        nc.gpsimd.tensor_scalar(out=dst, in0=src, scalar1=1.0, scalar2=0.0, op0=ALU.mult, op1=ALU.add)
+        w3_codes = held([P, H], U32, "w3_codes")
+        w3_planes = held([P, H], U8, "w3_planes")
+
+        h_rows = [held([P, PACK, N_TILE], BF16, "h_rows%d" % half) for half in range(HALVES)]
+        for n, (half, t) in enumerate(blocks):
+            f = f_sb[half, t]
+            nc.vector.tensor_tensor(out=f[:], in0=a_acc[half, t][:], in1=f[:], op=ALU.subtract)
+            nc.scalar.activation(out=f[:], in_=f[:], func=ACT.Square)
+            if 1 <= n <= PACK:
+                nc.scalar.activation(
+                    out=h_rows[0][:, n - 1, :], in_=f_sb[0, n - 1][:], func=ACT.Copy, scale=gain_sb[:, n - 1 : n]
+                )
+
+        nc.vector.quantize_mx(
+            out=w3_codes[:].bitcast(FP8X4), scales=w3_planes[:], in_=w3_grouped[:].rearrange("p t m j -> p (t m j)")
+        )
+
+        neg_g2 = [held([P, S], F32, "neg_g2_%d" % t) for t in range(PACK)]
+        g_acc = {}
+        h_grouped = [held([P, N_TILE, PACK], BF16, "h_grouped%d" % half) for half in range(HALVES)]
+
+        def interleave(copy, grouped, rows, cols):
+            copy(
+                out=grouped[:, cols, :].rearrange("p (c i) t -> p c t i", i=4),
+                in_=rows[:, :, cols].rearrange("p t (c i) -> p c t i", i=4),
+            )
+
+        def scale_rows(t):
+            nc.vector.tensor_scalar_mul(out=h_rows[1][:, t, :], in0=f_sb[1, t][:], scalar1=gain_sb[:, t : t + 1])
+
+        def third_product(half):
+            h_codes = ring.tile([P, N_TILE], U32, name="h_codes", align_bytes=64)
+            h_plane = ring.tile([P, N_TILE], U8, name="h_plane", align_bytes=64)
+            nc.vector.quantize_mx(
+                out=h_codes[:].bitcast(FP8X4), scales=h_plane[:], in_=h_grouped[half][:].rearrange("p n t -> p (n t)")
+            )
+            for t in range(PACK):
+                g_acc[half, t] = bank(half, t)
+                nc.tensor.matmul_mx(
+                    out=g_acc[half, t][:],
+                    lhsT=w3_codes[:, t * P : (t + 1) * P].bitcast(FP8X4),
+                    lhsT_scale=w3_planes[:, t * P : (t + 1) * P],
+                    rhs=h_codes[:].bitcast(FP8X4),
+                    rhs_scale=h_plane[:],
+                    start=True,
+                    stop=True,
+                )
+
+        def residual(half, t):
+            nc.vector.scalar_tensor_tensor(
+                out=neg_g2[t][:, half * N_TILE : (half + 1) * N_TILE],
+                in0=g_acc[half, t][:],
+                scalar=-1.0,
+                in1=f_sb[half, t][:],
+                op0=ALU.mult,
+                op1=ALU.subtract,
+            )
+
+        scale_rows(0)
+        interleave(nc.vector.tensor_copy, h_grouped[0], h_rows[0], slice(0, N_TILE))
+        scale_rows(1)
+        scale_rows(2)
+        third_product(0)
+        scale_rows(3)
+        interleave(nc.scalar.copy, h_grouped[1], h_rows[1], slice(0, N_TILE // 2))
+        interleave(nc.vector.tensor_copy, h_grouped[1], h_rows[1], slice(N_TILE // 2, N_TILE))
+        residual(0, 0)
+        third_product(1)
+        for t in range(1, PACK):
+            residual(0, t)
+
+        y = held([P, PACK, NP], F32, "y")
+        out_rows = out_0.rearrange("(p t) m -> p t m", t=PACK)
+        bounded = {}
+
+        def first_pick(t):
+            residual(1, t)
+            picked = ring.tile([P, NP], F32, name="picked")
+            nc.vector.tensor_copy(out=picked[:], in_=neg_g2[t][:].indirect(pos1_sb[:]))
+            bounded[t] = held([P, NP], F32, "bounded%d" % t)
+            nc.scalar.activation(out=bounded[t][:], in_=picked[:], func=ACT.Tanh, scale=-1.0)
+
+        def second_pick(t, cols):
+            nc.vector.tensor_tensor(
+                out=y[:, t, cols],
+                in0=neg_g2[t][:].indirect(pos2_sb[:, cols.start // 16 : cols.stop // 16]),
+                in1=bounded[t][:, cols],
+                op=ALU.add,
+            )
+
+        def store_rows(t):
+            nc.sync.dma_start(out=out_rows[:, t, :], in_=y[:, t, :])
+
+        whole, left, right = slice(0, NP), slice(0, NP // 2), slice(NP // 2, NP)
+        y_grouped = held([P, NP, PACK], BF16, "y_grouped")
+        y_codes = held([P, NP], I32, "y_codes")
+        y_plane = held([P, NP], U8, "y_plane")
+        out_words = out_1[0].rearrange("p m t -> p (m t)").bitcast(I32)
+
+        def quantise_result(cols):
+            nc.vector.quantize_mx(
+                out=y_codes[:, cols].bitcast(FP8X4),
+                scales=y_plane[:, cols],
+                in_=y_grouped[:, cols, :].rearrange("p n t -> p (n t)"),
+            )
+            nc.sync.dma_start(out=out_words[:, cols], in_=y_codes[:, cols])
+
+        first_pick(0)
+        first_pick(1)
+        second_pick(0, whole)
+        store_rows(0)
+        first_pick(2)
+        second_pick(1, whole)
+        store_rows(1)
+        first_pick(3)
+        second_pick(2, left)
+        second_pick(3, left)
+        interleave(nc.scalar.copy, y_grouped, y, left)
+        second_pick(2, right)
+        store_rows(2)
+        second_pick(3, right)
+        store_rows(3)
+        quantise_result(left)
+        interleave(nc.vector.tensor_copy, y_grouped, y, right)
+        quantise_result(right)
+        for q in range(QUADS):
+            engine = nc.scalar if q % 2 else nc.sync
+            engine.dma_start(
+                out=out_2[0, LIVE * q : LIVE * (q + 1), :].bitcast(I32),
+                in_=y_plane[QUAD * q : QUAD * q + LIVE, :].bitcast(I32),
+            )

@@ -49,7 +49,7 @@ def tile_list_hose_gauge_features_kernel(
         pos1_sb = lists.tile([P, NP // 16], U16, name="pos1_sb")
         pos2_sb = lists.tile([P, NP // 16], U16, name="pos2_sb")
 
-        tab_scale_win = placed([P, T], U8, "tab_scale_win", 46)
+        tab_scale_win = placed([P, T], U8, "tab_scale_win", 48)
         w2_scale_raw = held([P, PASSES, H], U8, "w2_scale_raw")
         v_planes = held([P, PASSES - 1, S], U8, "v_planes")
         nc.vector.memset(tab_scale_win[:].bitcast(I32), 0)
@@ -73,6 +73,7 @@ def tile_list_hose_gauge_features_kernel(
         nc.sync.dma_start(out=w2_raw[:].bitcast(I32), in_=w2_words.rearrange("a p c -> p a c").bitcast(I32))
         load_table(0)
         load_table(1)
+        load_table(2)
         nc.sync.dma_start(pos1_sb[:], pos1)
         nc.sync.dma_start(pos2_sb[:], pos2)
         for q in range(QUADS):
@@ -87,7 +88,7 @@ def tile_list_hose_gauge_features_kernel(
             )
         nc.sync.dma_start(out=gain_sb[:], in_=gain.rearrange("(p t) -> p t", t=PACK))
 
-        w2_codes = held([P, PACK, PASSES, 2 * P], U8, "w2_codes")
+        w2_codes = keep.tile([P, PACK, PASSES, 2 * P], U8, name="w2_codes", tag="late_weights", align_bytes=64)
         nc.vector.tensor_copy(
             out=w2_codes[:].rearrange("p t a (m b) -> p t a m b", b=2),
             in_=w2_raw[:].rearrange("p a (m t b) -> p t a m b", t=PACK, b=2),
@@ -112,7 +113,6 @@ def tile_list_hose_gauge_features_kernel(
         v_early = placed([P, (PASSES - 1) * S], U32, "v_early", 48)
         v_last = held([P, S], U32, "v_last")
         v_words = [v_early[:, a * S : (a + 1) * S] for a in range(PASSES - 1)] + [v_last[:]]
-        load_table(PASSES - 1)
         for a in range(PASSES - 1):
             nc.vector.tensor_copy(out=v_words[a], in_=tab_sb[a][:].bitcast(U32).indirect(offs_sb[:]))
         for a in range(PASSES - 1):
@@ -155,14 +155,17 @@ def tile_list_hose_gauge_features_kernel(
         def dealt_views(grouped, raw, m0):
             width = raw.shape[2] // PACK
             return (
-                grouped[:, :, m0 : m0 + width, :].rearrange("p t m j -> p m t j"),
-                raw[:].rearrange("p j (m t) -> p m t j", t=PACK),
+                grouped[:, :, m0 : m0 + width, :].rearrange("p (u e) m j -> p u m e j", e=2),
+                raw[:].rearrange("p j (m u e) -> p u m e j", u=2, e=2),
             )
 
         w1_codes = [held([P, H], U32, "w1_codes%d" % a) for a in range(PASSES)]
         w1_planes = [held([P, H], U8, "w1_planes%d" % a) for a in range(PASSES)]
         for a in range(PASSES):
-            grouped = ring.tile([P, PACK, P, PACK], BF16, name="w1_grouped", align_bytes=64)
+            if a < PASSES - 1:
+                grouped = ring.tile([P, PACK, P, PACK], BF16, name="w1_grouped", align_bytes=64)
+            else:
+                grouped = keep.tile([P, PACK, P, PACK], BF16, name="w1_grouped_last", tag="late_weights", align_bytes=64)
             pieces = [(w1_raw[a], 0)] if a < PASSES - 1 else [(w1_last[c], c * (P // 2)) for c in range(2)]
             for raw, m0 in pieces:
                 dst, src = dealt_views(grouped, raw, m0)
@@ -204,9 +207,10 @@ def tile_list_hose_gauge_features_kernel(
             for a in range(1, PASSES):
                 a_pass(a, half)
 
-        w3_grouped = held([P, PACK, P, PACK], BF16, "w3_grouped")
+        w3_grouped = keep.tile([P, PACK, P, PACK], BF16, name="w3_grouped", tag="late_weights", align_bytes=64)
         dst, src = dealt_views(w3_grouped, w3_raw, 0)
-        nc.gpsimd.tensor_scalar(out=dst, in0=src, scalar1=1.0, scalar2=0.0, op0=ALU.mult, op1=ALU.add)
+        for u in range(2):
+            nc.gpsimd.tensor_scalar(out=dst[:, u], in0=src[:, u], scalar1=1.0, scalar2=0.0, op0=ALU.mult, op1=ALU.add)
         w3_codes = held([P, H], U32, "w3_codes")
         w3_planes = held([P, H], U8, "w3_planes")
 

@@ -25,7 +25,8 @@ HALVES = S // N_TILE
 QUADS = 4
 QUAD = 32
 LIVE = 4
-SHIFT_ROWS = 112
+FIRST_ROW = QUAD - LIVE * PASSES
+SHIFT_ROWS = (104, 104, 100)
 
 
 def tile_list_hose_gauge_features_kernel(
@@ -49,11 +50,12 @@ def tile_list_hose_gauge_features_kernel(
         pos1_sb = lists.tile([P, NP // 16], U16, name="pos1_sb")
         pos2_sb = lists.tile([P, NP // 16], U16, name="pos2_sb")
 
-        tab_scale_win = placed([P, T], U8, "tab_scale_win", 48)
+        tab_scale_win = placed([P, T], U8, "tab_scale_win", 46)
         w2_scale_raw = held([P, PASSES, H], U8, "w2_scale_raw")
-        v_planes = held([P, PASSES - 1, S], U8, "v_planes")
-        nc.vector.memset(tab_scale_win[:].bitcast(I32), 0)
+        v_planes = held([P, PASSES, S], U8, "v_planes")
         nc.vector.memset(w2_scale_raw[:].rearrange("p a c -> p (a c)").bitcast(I32), 0)
+        for q in range(QUADS):
+            nc.vector.memset(tab_scale_win[QUAD * q : QUAD * q + FIRST_ROW, :].bitcast(I32), 0)
         nc.vector.memset(v_planes[:].rearrange("p a c -> p (a c)").bitcast(I32), 0)
 
         tab_sb = [placed([P, T], I32, "tab%d" % a, 16 * a) for a in range(PASSES)]
@@ -71,21 +73,21 @@ def tile_list_hose_gauge_features_kernel(
 
         nc.sync.dma_start(offs_sb[:], offs)
         nc.sync.dma_start(out=w2_raw[:].bitcast(I32), in_=w2_words.rearrange("a p c -> p a c").bitcast(I32))
-        load_table(0)
-        load_table(1)
-        load_table(2)
-        nc.sync.dma_start(pos1_sb[:], pos1)
-        nc.sync.dma_start(pos2_sb[:], pos2)
         for q in range(QUADS):
-            nc.gpsimd.dma_start(
-                out=tab_scale_win[QUAD * q : QUAD * q + LIVE * PASSES, :].bitcast(I32),
+            queue = nc.sync if q < QUADS // 2 else nc.scalar
+            queue.dma_start(
+                out=tab_scale_win[QUAD * q + FIRST_ROW : QUAD * (q + 1), :].bitcast(I32),
                 in_=tab_scales[:, LIVE * q : LIVE * (q + 1), :].bitcast(I32),
             )
+        load_table(0)
         for q in range(QUADS):
-            nc.gpsimd.dma_start(
+            nc.scalar.dma_start(
                 out=w2_scale_raw[QUAD * q : QUAD * q + LIVE, :, :].bitcast(I32),
                 in_=w2_scales[:, LIVE * q : LIVE * (q + 1), :].rearrange("a r c -> r a c").bitcast(I32),
             )
+        nc.sync.dma_start(pos1_sb[:], pos1)
+        nc.sync.dma_start(pos2_sb[:], pos2)
+        load_table(1)
         nc.sync.dma_start(out=gain_sb[:], in_=gain.rearrange("(p t) -> p t", t=PACK))
 
         w2_codes = keep.tile([P, PACK, PASSES, 2 * P], U8, name="w2_codes", tag="late_weights", align_bytes=64)
@@ -95,10 +97,12 @@ def tile_list_hose_gauge_features_kernel(
         )
         v_scale_packed = held([P, S], U8, "v_scale_packed")
         nc.vector.tensor_copy(out=v_scale_packed[:], in_=tab_scale_win[:].indirect(offs_sb[:]))
-        for a in range(1, PASSES):
-            nc.scalar.dma_start(
-                out=v_planes[0:SHIFT_ROWS, a - 1, :].bitcast(I32),
-                in_=v_scale_packed[LIVE * a : LIVE * a + SHIFT_ROWS, :].bitcast(I32),
+        for a in range(PASSES):
+            queue = nc.sync if a < PASSES - 1 else nc.scalar
+            first = FIRST_ROW + LIVE * a
+            queue.dma_start(
+                out=v_planes[0 : SHIFT_ROWS[a], a, :].bitcast(I32),
+                in_=v_scale_packed[first : first + SHIFT_ROWS[a], :].bitcast(I32),
             )
         w2_planes = held([P, PACK, PASSES, P], U8, "w2_planes")
         nc.vector.tensor_copy(
@@ -108,11 +112,12 @@ def tile_list_hose_gauge_features_kernel(
 
         def v_plane(a, half):
             cols = slice(half * N_TILE, (half + 1) * N_TILE)
-            return v_scale_packed[:, cols] if a == 0 else v_planes[:, a - 1, cols]
+            return v_planes[:, a, cols]
 
         v_early = placed([P, (PASSES - 1) * S], U32, "v_early", 48)
         v_last = held([P, S], U32, "v_last")
         v_words = [v_early[:, a * S : (a + 1) * S] for a in range(PASSES - 1)] + [v_last[:]]
+        load_table(PASSES - 1)
         for a in range(PASSES - 1):
             nc.vector.tensor_copy(out=v_words[a], in_=tab_sb[a][:].bitcast(U32).indirect(offs_sb[:]))
         for a in range(PASSES - 1):
@@ -215,14 +220,25 @@ def tile_list_hose_gauge_features_kernel(
         w3_planes = held([P, H], U8, "w3_planes")
 
         h_rows = [held([P, PACK, N_TILE], BF16, "h_rows%d" % half) for half in range(HALVES)]
+
+        def scale_rows(engine, half, t, on_scalar=False):
+            out, f, factor = h_rows[half][:, t, :], f_sb[half, t][:], gain_sb[:, t : t + 1]
+            if on_scalar:
+                engine.activation(out=out, in_=f, func=ACT.Copy, scale=factor)
+            else:
+                engine.tensor_scalar(out=out, in0=f, scalar1=factor, scalar2=0.0, op0=ALU.mult, op1=ALU.add)
+
         for n, (half, t) in enumerate(blocks):
             f = f_sb[half, t]
             nc.vector.tensor_tensor(out=f[:], in0=a_acc[half, t][:], in1=f[:], op=ALU.subtract)
             nc.scalar.activation(out=f[:], in_=f[:], func=ACT.Square)
-            if 1 <= n <= PACK:
-                nc.scalar.activation(
-                    out=h_rows[0][:, n - 1, :], in_=f_sb[0, n - 1][:], func=ACT.Copy, scale=gain_sb[:, n - 1 : n]
-                )
+            if n < 2:
+                scale_rows(nc.gpsimd, half, t)
+            if n == 3:
+                scale_rows(nc.scalar, 0, 2, True)
+                scale_rows(nc.scalar, 0, 3, True)
+        scale_rows(nc.scalar, 1, 2, True)
+        scale_rows(nc.scalar, 1, 3, True)
 
         nc.vector.quantize_mx(
             out=w3_codes[:].bitcast(FP8X4), scales=w3_planes[:], in_=w3_grouped[:].rearrange("p t m j -> p (t m j)")
@@ -237,9 +253,6 @@ def tile_list_hose_gauge_features_kernel(
                 out=grouped[:, cols, :].rearrange("p (c i) t -> p c t i", i=4),
                 in_=rows[:, :, cols].rearrange("p t (c i) -> p c t i", i=4),
             )
-
-        def scale_rows(t):
-            nc.vector.tensor_scalar_mul(out=h_rows[1][:, t, :], in0=f_sb[1, t][:], scalar1=gain_sb[:, t : t + 1])
 
         def third_product(half):
             h_codes = ring.tile([P, N_TILE], U32, name="h_codes", align_bytes=64)
@@ -269,18 +282,15 @@ def tile_list_hose_gauge_features_kernel(
                 op1=ALU.subtract,
             )
 
-        scale_rows(0)
         interleave(nc.vector.tensor_copy, h_grouped[0], h_rows[0], slice(0, N_TILE))
-        scale_rows(1)
-        scale_rows(2)
+        scale_rows(nc.vector, 1, 0)
         third_product(0)
-        scale_rows(3)
-        interleave(nc.scalar.copy, h_grouped[1], h_rows[1], slice(0, N_TILE // 2))
-        interleave(nc.vector.tensor_copy, h_grouped[1], h_rows[1], slice(N_TILE // 2, N_TILE))
-        residual(0, 0)
-        third_product(1)
-        for t in range(1, PACK):
+        scale_rows(nc.vector, 1, 1)
+        interleave(nc.scalar.copy, h_grouped[1], h_rows[1], slice(0, N_TILE))
+        for t in range(PACK - 1):
             residual(0, t)
+        third_product(1)
+        residual(0, PACK - 1)
 
         y = held([P, PACK, NP], F32, "y")
         out_rows = out_0.rearrange("(p t) m -> p t m", t=PACK)

@@ -25,8 +25,8 @@ HALVES = S // N_TILE
 QUADS = 4
 QUAD = 32
 LIVE = 4
-FIRST_ROW = QUAD - LIVE * PASSES
-SHIFT_ROWS = (104, 104, 100)
+ROWS = QUADS * LIVE
+SCALE_AT = (32, 48, 112)
 
 
 def tile_list_hose_gauge_features_kernel(
@@ -50,13 +50,13 @@ def tile_list_hose_gauge_features_kernel(
         pos1_sb = lists.tile([P, NP // 16], U16, name="pos1_sb")
         pos2_sb = lists.tile([P, NP // 16], U16, name="pos2_sb")
 
-        tab_scale_win = placed([P, T], U8, "tab_scale_win", 46)
+        tab_scale_win = placed([P, T], U8, "tab_scale_win", 30)
         w2_scale_raw = held([P, PASSES, H], U8, "w2_scale_raw")
         v_planes = held([P, PASSES, S], U8, "v_planes")
-        nc.vector.memset(w2_scale_raw[:].rearrange("p a c -> p (a c)").bitcast(I32), 0)
-        for q in range(QUADS):
-            nc.vector.memset(tab_scale_win[QUAD * q : QUAD * q + FIRST_ROW, :].bitcast(I32), 0)
-        nc.vector.memset(v_planes[:].rearrange("p a c -> p (a c)").bitcast(I32), 0)
+        nc.vector.memset(tab_scale_win[0:32, :].bitcast(I32), 0)
+        nc.vector.memset(tab_scale_win[64:112, :].bitcast(I32), 0)
+        nc.gpsimd.memset(w2_scale_raw[:].rearrange("p a c -> p (a c)").bitcast(I32), 0)
+        nc.gpsimd.memset(v_planes[:].rearrange("p a c -> p (a c)").bitcast(I32), 0)
 
         tab_sb = [placed([P, T], I32, "tab%d" % a, 16 * a) for a in range(PASSES)]
         w2_raw = held([P, PASSES, 2 * H], U8, "w2_raw")
@@ -71,39 +71,38 @@ def tile_list_hose_gauge_features_kernel(
         def w1_rows(a):
             return w1[a * K_PASS : (a + 1) * K_PASS, :].rearrange("(p j) c -> p j c", j=PACK)
 
+        scale_rows_hbm = tab_scales.rearrange("a q t -> (a q) t").bitcast(I32)
         nc.sync.dma_start(offs_sb[:], offs)
+        nc.sync.dma_start(out=tab_scale_win[32:64, :].bitcast(I32), in_=scale_rows_hbm[0:32, :])
+        nc.sync.dma_start(out=tab_scale_win[112:128, :].bitcast(I32), in_=scale_rows_hbm[32:48, :])
         nc.sync.dma_start(out=w2_raw[:].bitcast(I32), in_=w2_words.rearrange("a p c -> p a c").bitcast(I32))
-        for q in range(QUADS):
-            queue = nc.sync if q < QUADS // 2 else nc.scalar
-            queue.dma_start(
-                out=tab_scale_win[QUAD * q + FIRST_ROW : QUAD * (q + 1), :].bitcast(I32),
-                in_=tab_scales[:, LIVE * q : LIVE * (q + 1), :].bitcast(I32),
-            )
         load_table(0)
         for q in range(QUADS):
-            nc.scalar.dma_start(
+            nc.sync.dma_start(
                 out=w2_scale_raw[QUAD * q : QUAD * q + LIVE, :, :].bitcast(I32),
                 in_=w2_scales[:, LIVE * q : LIVE * (q + 1), :].rearrange("a r c -> r a c").bitcast(I32),
             )
         nc.sync.dma_start(pos1_sb[:], pos1)
         nc.sync.dma_start(pos2_sb[:], pos2)
-        load_table(1)
-        nc.sync.dma_start(out=gain_sb[:], in_=gain.rearrange("(p t) -> p t", t=PACK))
+        nc.gpsimd.dma_start(out=gain_sb[:], in_=gain.rearrange("(p t) -> p t", t=PACK))
 
-        w2_codes = keep.tile([P, PACK, PASSES, 2 * P], U8, name="w2_codes", tag="late_weights", align_bytes=64)
+        v_scale_packed = held([P, S], U8, "v_scale_packed")
+        nc.vector.tensor_copy(out=v_scale_packed[:], in_=tab_scale_win[:].indirect(offs_sb[:]))
+        load_table(1)
+        moves = [(a, q) for a in range(PASSES) for q in range(QUADS)]
+        for n, (a, q) in enumerate(moves):
+            if n == 6:
+                load_table(2)
+            first = SCALE_AT[a] + LIVE * q
+            nc.sync.dma_start(
+                out=v_planes[QUAD * q : QUAD * q + LIVE, a, :].bitcast(I32),
+                in_=v_scale_packed[first : first + LIVE, :].bitcast(I32),
+            )
+        w2_codes = held([P, PACK, PASSES, 2 * P], U8, "w2_codes")
         nc.vector.tensor_copy(
             out=w2_codes[:].rearrange("p t a (m b) -> p t a m b", b=2),
             in_=w2_raw[:].rearrange("p a (m t b) -> p t a m b", t=PACK, b=2),
         )
-        v_scale_packed = held([P, S], U8, "v_scale_packed")
-        nc.vector.tensor_copy(out=v_scale_packed[:], in_=tab_scale_win[:].indirect(offs_sb[:]))
-        for a in range(PASSES):
-            queue = nc.sync if a < PASSES - 1 else nc.scalar
-            first = FIRST_ROW + LIVE * a
-            queue.dma_start(
-                out=v_planes[0 : SHIFT_ROWS[a], a, :].bitcast(I32),
-                in_=v_scale_packed[first : first + SHIFT_ROWS[a], :].bitcast(I32),
-            )
         w2_planes = held([P, PACK, PASSES, P], U8, "w2_planes")
         nc.vector.tensor_copy(
             out=w2_planes[:],
@@ -114,10 +113,9 @@ def tile_list_hose_gauge_features_kernel(
             cols = slice(half * N_TILE, (half + 1) * N_TILE)
             return v_planes[:, a, cols]
 
-        v_early = placed([P, (PASSES - 1) * S], U32, "v_early", 48)
+        v_early = held([P, (PASSES - 1) * S], U32, "v_early")
         v_last = held([P, S], U32, "v_last")
         v_words = [v_early[:, a * S : (a + 1) * S] for a in range(PASSES - 1)] + [v_last[:]]
-        load_table(PASSES - 1)
         for a in range(PASSES - 1):
             nc.vector.tensor_copy(out=v_words[a], in_=tab_sb[a][:].bitcast(U32).indirect(offs_sb[:]))
         for a in range(PASSES - 1):
@@ -142,8 +140,9 @@ def tile_list_hose_gauge_features_kernel(
         blocks = [(half, t) for half in range(HALVES) for t in range(PACK)]
 
         b_acc = {blk: bank(*blk) for blk in blocks}
-        for a in range(PASSES):
-            for half, t in blocks:
+        b_order = [(0, blk) for blk in blocks] + [(a, blk) for blk in blocks for a in range(1, PASSES)]
+        for a, (half, t) in b_order:
+            if True:
                 nc.tensor.matmul_mx(
                     out=b_acc[half, t][:],
                     lhsT=w2_codes[:, t, a, :].bitcast(FP4X4),
@@ -154,8 +153,13 @@ def tile_list_hose_gauge_features_kernel(
                     stop=(a == PASSES - 1),
                 )
         f_sb = {(half, t): held([P, N_TILE], F32, "f%d_%d" % (half, t)) for half, t in blocks}
-        for blk in blocks:
+        early, late = blocks[:5], blocks[5:]
+
+        def magnitude(blk):
             nc.scalar.activation(out=f_sb[blk][:], in_=b_acc[blk][:], func=ACT.Abs)
+
+        for blk in early:
+            magnitude(blk)
 
         def dealt_views(grouped, raw, m0):
             width = raw.shape[2] // PACK
@@ -170,7 +174,7 @@ def tile_list_hose_gauge_features_kernel(
             if a < PASSES - 1:
                 grouped = ring.tile([P, PACK, P, PACK], BF16, name="w1_grouped", align_bytes=64)
             else:
-                grouped = keep.tile([P, PACK, P, PACK], BF16, name="w1_grouped_last", tag="late_weights", align_bytes=64)
+                grouped = held([P, PACK, P, PACK], BF16, "w1_grouped_last")
             pieces = [(w1_raw[a], 0)] if a < PASSES - 1 else [(w1_last[c], c * (P // 2)) for c in range(2)]
             for raw, m0 in pieces:
                 dst, src = dealt_views(grouped, raw, m0)
@@ -192,30 +196,31 @@ def tile_list_hose_gauge_features_kernel(
                         in_=grouped[:, 2 * u : 2 * u + 2].rearrange("p t m j -> p (t m j)"),
                     )
 
+        for blk in late:
+            magnitude(blk)
+
         a_acc = {blk: bank(*blk) for blk in blocks}
 
-        def a_pass(a, half):
-            for t in range(PACK):
-                nc.tensor.matmul_mx(
-                    out=a_acc[half, t][:],
-                    lhsT=w1_codes[a][:, t * P : (t + 1) * P].bitcast(FP8X4),
-                    lhsT_scale=w1_planes[a][:, t * P : (t + 1) * P],
-                    rhs=v_codes(a, half),
-                    rhs_scale=v_plane(a, half),
-                    start=(a == 0),
-                    stop=(a == PASSES - 1),
-                )
+        def a_pass(a, half, t):
+            nc.tensor.matmul_mx(
+                out=a_acc[half, t][:],
+                lhsT=w1_codes[a][:, t * P : (t + 1) * P].bitcast(FP8X4),
+                lhsT_scale=w1_planes[a][:, t * P : (t + 1) * P],
+                rhs=v_codes(a, half),
+                rhs_scale=v_plane(a, half),
+                start=(a == 0),
+                stop=(a == PASSES - 1),
+            )
 
-        for half in range(HALVES):
-            a_pass(0, half)
-        for half in range(HALVES):
-            for a in range(1, PASSES):
-                a_pass(a, half)
+        for a in range(PASSES):
+            for half, t in early:
+                a_pass(a, half, t)
+        for half, t in late:
+            for a in range(PASSES):
+                a_pass(a, half, t)
 
-        w3_grouped = keep.tile([P, PACK, P, PACK], BF16, name="w3_grouped", tag="late_weights", align_bytes=64)
+        w3_grouped = held([P, PACK, P, PACK], BF16, "w3_grouped")
         dst, src = dealt_views(w3_grouped, w3_raw, 0)
-        for u in range(2):
-            nc.gpsimd.tensor_scalar(out=dst[:, u], in0=src[:, u], scalar1=1.0, scalar2=0.0, op0=ALU.mult, op1=ALU.add)
         w3_codes = held([P, H], U32, "w3_codes")
         w3_planes = held([P, H], U8, "w3_planes")
 
@@ -232,17 +237,12 @@ def tile_list_hose_gauge_features_kernel(
             f = f_sb[half, t]
             nc.vector.tensor_tensor(out=f[:], in0=a_acc[half, t][:], in1=f[:], op=ALU.subtract)
             nc.scalar.activation(out=f[:], in_=f[:], func=ACT.Square)
-            if n < 2:
-                scale_rows(nc.gpsimd, half, t)
-            if n == 3:
-                scale_rows(nc.scalar, 0, 2, True)
-                scale_rows(nc.scalar, 0, 3, True)
+            if n in (1, 3):
+                scale_rows(nc.scalar, 0, n - 1, True)
+                scale_rows(nc.scalar, 0, n, True)
         scale_rows(nc.scalar, 1, 2, True)
         scale_rows(nc.scalar, 1, 3, True)
-
-        nc.vector.quantize_mx(
-            out=w3_codes[:].bitcast(FP8X4), scales=w3_planes[:], in_=w3_grouped[:].rearrange("p t m j -> p (t m j)")
-        )
+        nc.vector.tensor_copy(out=dst, in_=src)
 
         neg_g2 = [held([P, S], F32, "neg_g2_%d" % t) for t in range(PACK)]
         g_acc = {}
@@ -283,6 +283,9 @@ def tile_list_hose_gauge_features_kernel(
             )
 
         interleave(nc.vector.tensor_copy, h_grouped[0], h_rows[0], slice(0, N_TILE))
+        nc.vector.quantize_mx(
+            out=w3_codes[:].bitcast(FP8X4), scales=w3_planes[:], in_=w3_grouped[:].rearrange("p t m j -> p (t m j)")
+        )
         scale_rows(nc.vector, 1, 0)
         third_product(0)
         scale_rows(nc.vector, 1, 1)

@@ -114,7 +114,7 @@ def tile_list_hose_gauge_features_kernel(
             return v_planes[:, a, cols]
 
         v_early = held([P, (PASSES - 1) * S], U32, "v_early")
-        v_last = held([P, S], U32, "v_last")
+        v_last = keep.tile([P, S], U32, name="v_last", tag="last_pass", align_bytes=64)
         v_words = [v_early[:, a * S : (a + 1) * S] for a in range(PASSES - 1)] + [v_last[:]]
         for a in range(PASSES - 1):
             nc.vector.tensor_copy(out=v_words[a], in_=tab_sb[a][:].bitcast(U32).indirect(offs_sb[:]))
@@ -152,8 +152,10 @@ def tile_list_hose_gauge_features_kernel(
                     start=(a == 0),
                     stop=(a == PASSES - 1),
                 )
-        f_sb = {(half, t): held([P, N_TILE], F32, "f%d_%d" % (half, t)) for half, t in blocks}
-        early, late = blocks[:5], blocks[5:]
+        f_sb = {(half, t): held([P, N_TILE], F32, "f%d_%d" % (half, t)) for half, t in blocks[:6]}
+        for n, (half, t) in enumerate(blocks[6:]):
+            f_sb[half, t] = placed([P, N_TILE], F32, "f%d_%d" % (half, t), 16 + 2 * n)
+        early, late = blocks[:6], blocks[6:]
 
         def magnitude(blk):
             nc.scalar.activation(out=f_sb[blk][:], in_=b_acc[blk][:], func=ACT.Abs)
@@ -219,7 +221,7 @@ def tile_list_hose_gauge_features_kernel(
             for a in range(PASSES):
                 a_pass(a, half, t)
 
-        w3_grouped = held([P, PACK, P, PACK], BF16, "w3_grouped")
+        w3_grouped = keep.tile([P, PACK, P, PACK], BF16, name="w3_grouped", tag="last_pass", align_bytes=64)
         dst, src = dealt_views(w3_grouped, w3_raw, 0)
         w3_codes = held([P, H], U32, "w3_codes")
         w3_planes = held([P, H], U8, "w3_planes")
@@ -237,9 +239,12 @@ def tile_list_hose_gauge_features_kernel(
             f = f_sb[half, t]
             nc.vector.tensor_tensor(out=f[:], in0=a_acc[half, t][:], in1=f[:], op=ALU.subtract)
             nc.scalar.activation(out=f[:], in_=f[:], func=ACT.Square)
-            if n in (1, 3):
+            if n < 2:
+                scale_rows(nc.gpsimd, 0, n)
+            if n == 3:
                 scale_rows(nc.scalar, 0, n - 1, True)
                 scale_rows(nc.scalar, 0, n, True)
+        scale_rows(nc.scalar, 1, 1, True)
         scale_rows(nc.scalar, 1, 2, True)
         scale_rows(nc.scalar, 1, 3, True)
         nc.vector.tensor_copy(out=dst, in_=src)
@@ -286,9 +291,8 @@ def tile_list_hose_gauge_features_kernel(
         nc.vector.quantize_mx(
             out=w3_codes[:].bitcast(FP8X4), scales=w3_planes[:], in_=w3_grouped[:].rearrange("p t m j -> p (t m j)")
         )
-        scale_rows(nc.vector, 1, 0)
         third_product(0)
-        scale_rows(nc.vector, 1, 1)
+        scale_rows(nc.vector, 1, 0)
         interleave(nc.scalar.copy, h_grouped[1], h_rows[1], slice(0, N_TILE))
         for t in range(PACK - 1):
             residual(0, t)
@@ -299,8 +303,13 @@ def tile_list_hose_gauge_features_kernel(
         out_rows = out_0.rearrange("(p t) m -> p t m", t=PACK)
         bounded = {}
 
+        for t in range(1, PACK):
+            product = ring.tile([P, N_TILE], F32, name="product", bufs=3)
+            nc.scalar.activation(out=product[:], in_=g_acc[1, t][:], func=ACT.Copy, scale=-1.0)
+            nc.gpsimd.tensor_tensor(out=neg_g2[t][:, N_TILE:S], in0=product[:], in1=f_sb[1, t][:], op=ALU.subtract)
+        residual(1, 0)
+
         def first_pick(t):
-            residual(1, t)
             picked = ring.tile([P, NP], F32, name="picked")
             nc.vector.tensor_copy(out=picked[:], in_=neg_g2[t][:].indirect(pos1_sb[:]))
             bounded[t] = held([P, NP], F32, "bounded%d" % t)
@@ -333,12 +342,12 @@ def tile_list_hose_gauge_features_kernel(
 
         first_pick(0)
         first_pick(1)
+        first_pick(2)
         second_pick(0, whole)
         store_rows(0)
-        first_pick(2)
+        first_pick(3)
         second_pick(1, whole)
         store_rows(1)
-        first_pick(3)
         second_pick(2, left)
         second_pick(3, left)
         interleave(nc.scalar.copy, y_grouped, y, left)

from contextlib import ExitStack

import concourse.mybir as mybir

K, H, T, S, NP = 1536, 512, 4096, 1024, 512
FLOPS = 2 * (2 * K * H * S + H * H * S)

F32 = mybir.dt.float32
BF16 = mybir.dt.bfloat16
I32 = mybir.dt.int32
U32 = mybir.dt.uint32
U16 = mybir.dt.uint16
U8 = mybir.dt.uint8
FP8X4 = mybir.dt.float8_e4m3fn_x4
FP4X4 = mybir.dt.float4_e2m1fn_x4
ALU = mybir.AluOpType
ACT = mybir.ActivationFunctionType

P = 128
PACK = 4
K_PASS = P * PACK
PASSES = K // K_PASS
N_TILE = 512
HALVES = S // N_TILE
QUADS = 4
QUAD = 32
LIVE = 4
ROWS = QUADS * LIVE
SCALE_AT = (32, 48, 112)


def tile_list_hose_gauge_features_kernel(
    tc, tab_words, tab_scales, w1, w2_words, w2_scales, gain, w3, offs, pos1, pos2, out_0, out_1, out_2
):
    nc = tc.nc
    with ExitStack() as ctx:
        lists = ctx.enter_context(tc.tile_pool(name="lists", bufs=1))
        keep = ctx.enter_context(tc.tile_pool(name="keep", bufs=1))
        ring = ctx.enter_context(tc.tile_pool(name="ring", bufs=2))
        reuse = ctx.enter_context(tc.tile_pool(name="reuse", bufs=1))
        psum = ctx.enter_context(tc.psum_pool(name="psum", bufs=1))

        def held(shape, dtype, name):
            return keep.tile(shape, dtype, name=name, align_bytes=64)

        def placed(shape, dtype, name, kib):
            return reuse.tile(shape, dtype, name=name, align_bytes=64, offset=kib * 1024)

        offs_sb = lists.tile([P, S // 16], U16, name="offs_sb")
        pos1_sb = lists.tile([P, NP // 16], U16, name="pos1_sb")
        pos2_sb = lists.tile([P, NP // 16], U16, name="pos2_sb")

        tab_scale_win = placed([P, T], U8, "tab_scale_win", 30)
        w2_scale_raw = held([P, PASSES, H], U8, "w2_scale_raw")
        v_planes = held([P, PASSES, S], U8, "v_planes")
        nc.vector.memset(tab_scale_win[0:32, :].bitcast(I32), 0)
        nc.vector.memset(tab_scale_win[64:112, :].bitcast(I32), 0)
        nc.gpsimd.memset(w2_scale_raw[:].rearrange("p a c -> p (a c)").bitcast(I32), 0)
        nc.gpsimd.memset(v_planes[:].rearrange("p a c -> p (a c)").bitcast(I32), 0)

        tab_sb = [placed([P, T], I32, "tab%d" % a, 16 * a) for a in range(PASSES)]
        w2_raw = held([P, PASSES, 2 * H], U8, "w2_raw")
        gain_sb = held([P, PACK], F32, "gain_sb")
        w1_raw = [placed([P, PACK, H], F32, "w1_raw%d" % a, 8 * a) for a in range(PASSES - 1)]
        w1_last = [placed([P, PACK, H // 2], F32, "w1_last%d" % c, 16 + 4 * c) for c in range(2)]
        w3_raw = placed([P, PACK, H], F32, "w3_raw", 24)

        def load_table(a):
            nc.sync.dma_start(out=tab_sb[a][:], in_=tab_words[a].rearrange("p t i -> p (t i)").bitcast(I32))

        def w1_rows(a):
            return w1[a * K_PASS : (a + 1) * K_PASS, :].rearrange("(p j) c -> p j c", j=PACK)

        scale_rows_hbm = tab_scales.rearrange("a q t -> (a q) t").bitcast(I32)
        nc.sync.dma_start(offs_sb[:], offs)
        nc.sync.dma_start(out=tab_scale_win[32:64, :].bitcast(I32), in_=scale_rows_hbm[0:32, :])
        nc.sync.dma_start(out=tab_scale_win[112:128, :].bitcast(I32), in_=scale_rows_hbm[32:48, :])
        nc.sync.dma_start(out=w2_raw[:].bitcast(I32), in_=w2_words.rearrange("a p c -> p a c").bitcast(I32))
        load_table(0)
        for q in range(QUADS):
            nc.sync.dma_start(
                out=w2_scale_raw[QUAD * q : QUAD * q + LIVE, :, :].bitcast(I32),
                in_=w2_scales[:, LIVE * q : LIVE * (q + 1), :].rearrange("a r c -> r a c").bitcast(I32),
            )
        nc.sync.dma_start(pos1_sb[:], pos1)
        nc.sync.dma_start(pos2_sb[:], pos2)
        nc.gpsimd.dma_start(out=gain_sb[:], in_=gain.rearrange("(p t) -> p t", t=PACK))

        v_scale_packed = held([P, S], U8, "v_scale_packed")
        nc.vector.tensor_copy(out=v_scale_packed[:], in_=tab_scale_win[:].indirect(offs_sb[:]))
        load_table(1)
        moves = [(a, q) for a in range(PASSES) for q in range(QUADS)]
        for n, (a, q) in enumerate(moves):
            if n == 6:
                load_table(2)
            first = SCALE_AT[a] + LIVE * q
            nc.sync.dma_start(
                out=v_planes[QUAD * q : QUAD * q + LIVE, a, :].bitcast(I32),
                in_=v_scale_packed[first : first + LIVE, :].bitcast(I32),
            )
        w2_codes = held([P, PACK, PASSES, 2 * P], U8, "w2_codes")
        nc.vector.tensor_copy(
            out=w2_codes[:].rearrange("p t a (m b) -> p t a m b", b=2),
            in_=w2_raw[:].rearrange("p a (m t b) -> p t a m b", t=PACK, b=2),
        )
        w2_planes = held([P, PACK, PASSES, P], U8, "w2_planes")
        nc.vector.tensor_copy(
            out=w2_planes[:],
            in_=w2_scale_raw[:].rearrange("p a (m t) -> p t a m", t=PACK),
        )

        def v_plane(a, half):
            cols = slice(half * N_TILE, (half + 1) * N_TILE)
            return v_planes[:, a, cols]

        v_early = held([P, (PASSES - 1) * S], U32, "v_early")
        v_last = keep.tile([P, S], U32, name="v_last", tag="last_pass", align_bytes=64)
        v_words = [v_early[:, a * S : (a + 1) * S] for a in range(PASSES - 1)] + [v_last[:]]
        for a in range(PASSES - 1):
            nc.vector.tensor_copy(out=v_words[a], in_=tab_sb[a][:].bitcast(U32).indirect(offs_sb[:]))
        for a in range(PASSES - 1):
            nc.sync.dma_start(out=w1_raw[a][:], in_=w1_rows(a))
        for c in range(2):
            nc.sync.dma_start(out=w1_last[c][:], in_=w1_rows(PASSES - 1)[:, :, c * (H // 2) : (c + 1) * (H // 2)])
        nc.sync.dma_start(out=w3_raw[:], in_=w3.rearrange("(p j) c -> p j c", j=PACK))
        for half in range(HALVES):
            nc.vector.tensor_copy(
                out=v_last[:, half * N_TILE : (half + 1) * N_TILE],
                in_=tab_sb[PASSES - 1][:]
                .bitcast(U32)
                .indirect(offs_sb[:, half * (N_TILE // 16) : (half + 1) * (N_TILE // 16)]),
            )

        def v_codes(a, half):
            return v_words[a][:, half * N_TILE : (half + 1) * N_TILE].bitcast(FP8X4)

        def bank(half, t):
            return psum.tile([P, N_TILE], F32, name="bank", tag="bank%d_%d" % (half, t))

        blocks = [(half, t) for half in range(HALVES) for t in range(PACK)]

        b_acc = {blk: bank(*blk) for blk in blocks}
        b_order = [(0, blk) for blk in blocks] + [(a, blk) for blk in blocks for a in range(1, PASSES)]
        for a, (half, t) in b_order:
            if True:
                nc.tensor.matmul_mx(
                    out=b_acc[half, t][:],
                    lhsT=w2_codes[:, t, a, :].bitcast(FP4X4),
                    lhsT_scale=w2_planes[:, t, a, :],
                    rhs=v_codes(a, half),
                    rhs_scale=v_plane(a, half),
                    start=(a == 0),
                    stop=(a == PASSES - 1),
                )
        f_sb = {(half, t): held([P, N_TILE], F32, "f%d_%d" % (half, t)) for half, t in blocks[:6]}
        for n, (half, t) in enumerate(blocks[6:]):
            f_sb[half, t] = placed([P, N_TILE], F32, "f%d_%d" % (half, t), 16 + 2 * n)
        early, late = blocks[:6], blocks[6:]

        def magnitude(blk):
            nc.scalar.activation(out=f_sb[blk][:], in_=b_acc[blk][:], func=ACT.Abs)

        for blk in early:
            magnitude(blk)

        def dealt_views(grouped, raw, m0):
            width = raw.shape[2] // PACK
            return (
                grouped[:, :, m0 : m0 + width, :].rearrange("p (u e) m j -> p u m e j", e=2),
                raw[:].rearrange("p j (m u e) -> p u m e j", u=2, e=2),
            )

        w1_codes = [held([P, H], U32, "w1_codes%d" % a) for a in range(PASSES)]
        w1_planes = [held([P, H], U8, "w1_planes%d" % a) for a in range(PASSES)]
        for a in range(PASSES):
            if a < PASSES - 1:
                grouped = ring.tile([P, PACK, P, PACK], BF16, name="w1_grouped", align_bytes=64)
            else:
                grouped = held([P, PACK, P, PACK], BF16, "w1_grouped_last")
            pieces = [(w1_raw[a], 0)] if a < PASSES - 1 else [(w1_last[c], c * (P // 2)) for c in range(2)]
            for raw, m0 in pieces:
                dst, src = dealt_views(grouped, raw, m0)
                if a == PASSES - 1 and m0 == 0:
                    nc.scalar.copy(out=dst, in_=src)
                else:
                    nc.vector.tensor_copy(out=dst, in_=src)
            if a < PASSES - 1:
                nc.vector.quantize_mx(
                    out=w1_codes[a][:].bitcast(FP8X4),
                    scales=w1_planes[a][:],
                    in_=grouped[:].rearrange("p t m j -> p (t m j)"),
                )
            else:
                for u in range(2):
                    nc.vector.quantize_mx(
                        out=w1_codes[a][:, u * 2 * P : (u + 1) * 2 * P].bitcast(FP8X4),
                        scales=w1_planes[a][:, u * 2 * P : (u + 1) * 2 * P],
                        in_=grouped[:, 2 * u : 2 * u + 2].rearrange("p t m j -> p (t m j)"),
                    )

        for blk in late:
            magnitude(blk)

        a_acc = {blk: bank(*blk) for blk in blocks}

        def a_pass(a, half, t):
            nc.tensor.matmul_mx(
                out=a_acc[half, t][:],
                lhsT=w1_codes[a][:, t * P : (t + 1) * P].bitcast(FP8X4),
                lhsT_scale=w1_planes[a][:, t * P : (t + 1) * P],
                rhs=v_codes(a, half),
                rhs_scale=v_plane(a, half),
                start=(a == 0),
                stop=(a == PASSES - 1),
            )

        for a in range(PASSES):
            for half, t in early:
                a_pass(a, half, t)
        for half, t in late:
            for a in range(PASSES):
                a_pass(a, half, t)

        w3_grouped = keep.tile([P, PACK, P, PACK], BF16, name="w3_grouped", tag="last_pass", align_bytes=64)
        dst, src = dealt_views(w3_grouped, w3_raw, 0)
        w3_codes = held([P, H], U32, "w3_codes")
        w3_planes = held([P, H], U8, "w3_planes")

        h_rows = [held([P, PACK, N_TILE], BF16, "h_rows%d" % half) for half in range(HALVES)]

        def scale_rows(engine, half, t, on_scalar=False):
            out, f, factor = h_rows[half][:, t, :], f_sb[half, t][:], gain_sb[:, t : t + 1]
            if on_scalar:
                engine.activation(out=out, in_=f, func=ACT.Copy, scale=factor)
            else:
                engine.tensor_scalar(out=out, in0=f, scalar1=factor, scalar2=0.0, op0=ALU.mult, op1=ALU.add)

        for n, (half, t) in enumerate(blocks):
            f = f_sb[half, t]
            nc.vector.tensor_tensor(out=f[:], in0=a_acc[half, t][:], in1=f[:], op=ALU.subtract)
            nc.scalar.activation(out=f[:], in_=f[:], func=ACT.Square)
            if n < 2:
                scale_rows(nc.gpsimd, 0, n)
            if n == 3:
                scale_rows(nc.scalar, 0, n - 1, True)
                scale_rows(nc.scalar, 0, n, True)
        scale_rows(nc.scalar, 1, 1, True)
        scale_rows(nc.scalar, 1, 2, True)
        scale_rows(nc.scalar, 1, 3, True)
        nc.vector.tensor_copy(out=dst, in_=src)

        neg_g2 = [held([P, S], F32, "neg_g2_%d" % t) for t in range(PACK)]
        g_acc = {}
        h_grouped = [held([P, N_TILE, PACK], BF16, "h_grouped%d" % half) for half in range(HALVES)]

        def interleave(copy, grouped, rows, cols):
            copy(
                out=grouped[:, cols, :].rearrange("p (c i) t -> p c t i", i=4),
                in_=rows[:, :, cols].rearrange("p t (c i) -> p c t i", i=4),
            )

        def third_product(half):
            h_codes = ring.tile([P, N_TILE], U32, name="h_codes", align_bytes=64)
            h_plane = ring.tile([P, N_TILE], U8, name="h_plane", align_bytes=64)
            nc.vector.quantize_mx(
                out=h_codes[:].bitcast(FP8X4), scales=h_plane[:], in_=h_grouped[half][:].rearrange("p n t -> p (n t)")
            )
            for t in range(PACK):
                g_acc[half, t] = bank(half, t)
                nc.tensor.matmul_mx(
                    out=g_acc[half, t][:],
                    lhsT=w3_codes[:, t * P : (t + 1) * P].bitcast(FP8X4),
                    lhsT_scale=w3_planes[:, t * P : (t + 1) * P],
                    rhs=h_codes[:].bitcast(FP8X4),
                    rhs_scale=h_plane[:],
                    start=True,
                    stop=True,
                )

        def residual(half, t):
            nc.vector.scalar_tensor_tensor(
                out=neg_g2[t][:, half * N_TILE : (half + 1) * N_TILE],
                in0=g_acc[half, t][:],
                scalar=-1.0,
                in1=f_sb[half, t][:],
                op0=ALU.mult,
                op1=ALU.subtract,
            )

        interleave(nc.vector.tensor_copy, h_grouped[0], h_rows[0], slice(0, N_TILE))
        nc.vector.quantize_mx(
            out=w3_codes[:].bitcast(FP8X4), scales=w3_planes[:], in_=w3_grouped[:].rearrange("p t m j -> p (t m j)")
        )
        third_product(0)
        scale_rows(nc.vector, 1, 0)
        interleave(nc.scalar.copy, h_grouped[1], h_rows[1], slice(0, N_TILE))
        for t in range(PACK - 1):
            residual(0, t)
        third_product(1)
        residual(0, PACK - 1)

        y = held([P, PACK, NP], F32, "y")
        out_rows = out_0.rearrange("(p t) m -> p t m", t=PACK)
        bounded = {}

        for t in range(1, PACK):
            product = ring.tile([P, N_TILE], F32, name="product", bufs=3)
            nc.scalar.activation(out=product[:], in_=g_acc[1, t][:], func=ACT.Copy, scale=-1.0)
            nc.gpsimd.tensor_tensor(out=neg_g2[t][:, N_TILE:S], in0=product[:], in1=f_sb[1, t][:], op=ALU.subtract)
        residual(1, 0)

        def first_pick(t):
            picked = ring.tile([P, NP], F32, name="picked")
            nc.vector.tensor_copy(out=picked[:], in_=neg_g2[t][:].indirect(pos1_sb[:]))
            bounded[t] = held([P, NP], F32, "bounded%d" % t)
            nc.scalar.activation(out=bounded[t][:], in_=picked[:], func=ACT.Tanh, scale=-1.0)

        def second_pick(t, cols):
            nc.vector.tensor_tensor(
                out=y[:, t, cols],
                in0=neg_g2[t][:].indirect(pos2_sb[:, cols.start // 16 : cols.stop // 16]),
                in1=bounded[t][:, cols],
                op=ALU.add,
            )

        def store_rows(t):
            nc.sync.dma_start(out=out_rows[:, t, :], in_=y[:, t, :])

        whole, left, right = slice(0, NP), slice(0, NP // 2), slice(NP // 2, NP)
        y_grouped = held([P, NP, PACK], BF16, "y_grouped")
        y_codes = held([P, NP], I32, "y_codes")
        y_plane = held([P, NP], U8, "y_plane")
        out_words = out_1[0].rearrange("p m t -> p (m t)").bitcast(I32)

        def quantise_result(cols):
            nc.vector.quantize_mx(
                out=y_codes[:, cols].bitcast(FP8X4),
                scales=y_plane[:, cols],
                in_=y_grouped[:, cols, :].rearrange("p n t -> p (n t)"),
            )
            nc.sync.dma_start(out=out_words[:, cols], in_=y_codes[:, cols])

        first_pick(0)
        first_pick(1)
        first_pick(2)
        second_pick(0, whole)
        store_rows(0)
        first_pick(3)
        second_pick(1, whole)
        store_rows(1)
        second_pick(2, left)
        second_pick(3, left)
        interleave(nc.scalar.copy, y_grouped, y, left)
        second_pick(2, right)
        store_rows(2)
        second_pick(3, right)
        store_rows(3)
        quantise_result(left)
        interleave(nc.vector.tensor_copy, y_grouped, y, right)
        quantise_result(right)
        for q in range(QUADS):
            engine = nc.scalar if q % 2 else nc.sync
            engine.dma_start(
                out=out_2[0, LIVE * q : LIVE * (q + 1), :].bitcast(I32),
                in_=y_plane[QUAD * q : QUAD * q + LIVE, :].bitcast(I32),
            )
